import numpy as np
import ml_dtypes


def mxq(x, axis, fmt="e4m3"):
    dtype, down = {"e4m3": (ml_dtypes.float8_e4m3fn, 7), "e5m2": (ml_dtypes.float8_e5m2, 14)}[fmt]
    v = np.moveaxis(np.asarray(x, np.float32).astype(ml_dtypes.bfloat16).astype(np.float64), axis, -1)
    blocks = v.reshape(v.shape[:-1] + (-1, 32))
    amax = np.abs(blocks).max(-1, keepdims=True)
    byte = np.maximum(np.where(amax > 0, np.frexp(amax)[1] - 1 + 127, 0) - down, 1)
    scale = np.exp2(byte - 127.0)
    codes = (blocks / scale).astype(np.float32).astype(dtype).astype(np.float64)
    return np.moveaxis((codes * scale).reshape(v.shape), -1, axis)


WIDE = False


def mx_kscale(k):
    if not WIDE:
        return np.ones(k)
    levels = np.array([10, -10, 5, -5, 0])
    if k % 512:
        return np.exp2(np.random.permutation(np.resize(levels, k // 32))).repeat(32)
    a = np.empty((k // 512, 16))
    for p in range(k // 512):
        a[p, :8] = np.random.permutation(np.resize(levels, 8))
        for g in range(8):
            far = levels[np.abs(levels - a[p, g]) >= 10]
            a[p, g + 8] = far[np.random.randint(len(far))]
    return np.exp2(a.ravel()).repeat(32)


def f64(x):
    return np.asarray(x).astype(np.float64)


def striped(idx):
    return np.tile(idx.reshape(-1, 16).T, (8, 1)).astype(np.uint16)


def unstriped(offs):
    return offs[:16].T.reshape(-1).astype(np.int64)


E2M1 = np.array([0.0, 0.5, 1.0, 1.5, 2.0, 3.0, 4.0, 6.0, -0.0, -0.5, -1.0, -1.5, -2.0, -3.0, -4.0, -6.0])


def pack_weight(w, fmt):
    k, n = w.shape
    w = f64(np.asarray(w, np.float32).astype(ml_dtypes.bfloat16)).reshape(k // 32, 32, n)
    amax = np.abs(w).max(1)
    if fmt == "e4m3":
        byte = np.frexp(amax)[1] - 1 + 127 - 7
    else:
        mant, ex = np.frexp(amax / 6.0)
        byte = np.where(mant > 0.5, ex, ex - 1) + 127
    byte = np.clip(np.where(amax > 0, byte, 1), 1, 254)
    scaled = (w * np.exp2(127.0 - byte)[:, None, :]).reshape(k, n).astype(np.float32)
    by_word = np.ascontiguousarray(scaled.reshape(k // 512, 128, 4, n).transpose(0, 1, 3, 2))
    if fmt == "e4m3":
        words = by_word.astype(ml_dtypes.float8_e4m3fn).view(np.uint8)
    else:
        c = by_word.astype(ml_dtypes.float4_e2m1fn).view(np.uint8) & 0xF
        words = (c[..., 0::2] | (c[..., 1::2] << 4)).reshape(k // 512, 128, 2 * n)
    return np.ascontiguousarray(words), np.ascontiguousarray(byte.astype(np.uint8).reshape(k // 512, 16, n))


def unpack_weight(words, scales, fmt):
    g, _, n = scales.shape
    words = np.ascontiguousarray(words).reshape(g, 128, n, -1)
    if fmt == "e4m3":
        vals = words.view(ml_dtypes.float8_e4m3fn).astype(np.float64)
    else:
        nib = np.empty((g, 128, n, 4), np.uint8)
        nib[..., 0::2] = words & 0xF
        nib[..., 1::2] = words >> 4
        vals = E2M1[nib]
    vals = vals * np.repeat(np.exp2(scales.astype(np.float64) - 127.0), 8, axis=1)[..., None]
    return vals.transpose(0, 1, 3, 2).reshape(g * 512, n)


def silu(v):
    return v / (1.0 + np.exp(-np.maximum(v, -700.0)))


K, T, E, N = 2048, 768, 2, 384
COUNTS = (256, 512)
STARTS = np.cumsum((0,) + COUNTS)


def by_expert(wq, xq):
    return np.concatenate([wq[e].T @ xq[:, STARTS[e]:STARTS[e + 1]] for e in range(E)], axis=1)


def setup_inputs():
    n = np.random.standard_normal
    s = mx_kscale(K)[:, None]
    expert = np.random.permutation(np.repeat(np.arange(E), COUNTS))
    slot_token = np.argsort(expert, kind="stable")
    w = [pack_weight(m, "e2m1") for m in n((E, K, N)) / np.sqrt(K) / s[None]]
    return {
        "xT": (n((K, T)) * s).astype(np.float32),
        "w_words": np.stack([m[0] for m in w]),
        "w_scales": np.stack([m[1] for m in w]),
        "b": (0.3 * n((N, E))).astype(np.float32),
        "gate": np.tile(np.random.uniform(0.2, 1.0, T), (N, 1)).astype(np.float32),
        "offs": striped(slot_token),
    }


def reference(xT, w_words, w_scales, b, gate, offs):
    idx = unstriped(offs)
    w = np.stack([unpack_weight(w_words[e], w_scales[e], "e2m1") for e in range(E)])
    xq = mxq(f64(xT)[:, idx], 0, "e4m3")
    y = by_expert(w, xq)
    y = silu(y + np.repeat(f64(b), COUNTS, axis=1))
    out = np.zeros((N, T))
    out[:, idx] = f64(gate) * y
    return out

@@ -1,0 +1,153 @@
+import concourse.mybir as mybir
+
+K, T, E, N = 2048, 768, 2, 384
+COUNTS = (256, 512)
+STARTS = (0, 256)
+FLOPS = 2 * T * K * N
+
+P = 128
+PACK = 4
+K_PASS = P * PACK
+PASSES = K // K_PASS
+N_BLOCKS = N // P
+WINDOW = 1024
+
+F32 = mybir.dt.float32
+BF16 = mybir.dt.bfloat16
+I32 = mybir.dt.int32
+U32 = mybir.dt.uint32
+U16 = mybir.dt.uint16
+U8 = mybir.dt.uint8
+E4M3X4 = mybir.dt.float8_e4m3fn_x4
+E2M1X4 = mybir.dt.float4_e2m1fn_x4
+COPY = mybir.ActivationFunctionType.Copy
+SILU = mybir.ActivationFunctionType.Silu
+MULT = mybir.AluOpType.mult
+
+LOADS = ((0, 256, 768), (0, 768), (0, 768), (0, 512, 768))
+CASTS = (
+    (("v", 0, 256), ("s", 256, 512), ("v", 512, 768)),
+    (("s", 0, 256), ("s", 256, 512), ("s", 512, 768)),
+    (("s", 0, 256), ("s", 256, 512), ("s", 512, 768)),
+    (("s", 0, 256), ("v", 256, 512), ("v", 512, 640), ("s", 640, 768)),
+)
+QUANTS = ((0, 256), (256, 512), (512, 768))
+
+
+def tile_moe_rag_lin_silu_kernel(tc, xT, w_words, w_scales, b, gate, offs, out):
+    nc = tc.nc
+    with tc.tile_pool(name="keep", bufs=1) as keep, tc.psum_pool(name="psum", bufs=1) as psum:
+        offsets = keep.tile([P, T // 16], U16, name="offsets")
+        raw = [keep.tile([P, PACK, T], F32, name="raw%d" % a, align_bytes=64) for a in range(PASSES)]
+        grouped = [keep.tile([P, T, PACK], BF16, name="grouped%d" % a, align_bytes=64) for a in range(PASSES)]
+        words = [keep.tile([P, T], U32, name="words%d" % a, align_bytes=64) for a in range(PASSES)]
+        scales = keep.tile([P, PASSES, T], U8, name="scales", align_bytes=64)
+        slot_words = [keep.tile([P, T], U32, name="slot_words%d" % a, align_bytes=64) for a in range(PASSES)]
+        slot_scales = [keep.tile([P, T], U8, name="slot_scales%d" % a, align_bytes=64) for a in range(PASSES)]
+        w_codes = [keep.tile([P, E, 2 * N], U8, name="w_codes%d" % a, align_bytes=64) for a in range(PASSES)]
+        w_planes = keep.tile([P, E * PASSES, N], U8, name="w_planes", align_bytes=64)
+        bias = keep.tile([P, N_BLOCKS, E], F32, name="bias")
+        gates = keep.tile([P, N_BLOCKS, T], F32, name="gates")
+        probe = keep.tile([P, 1], F32, name="probe")
+        y = [keep.tile([P, T], F32, name="y%d" % n) for n in range(N_BLOCKS)]
+        spread = [keep.tile([P, WINDOW], F32, name="spread%d" % n) for n in range(N_BLOCKS)]
+        acc0 = [psum.tile([P, COUNTS[0]], F32, name="acc0_%d" % n) for n in range(N_BLOCKS)]
+        acc1 = [psum.tile([P, COUNTS[1]], F32, name="acc1_%d" % n) for n in range(N_BLOCKS)]
+
+        nc.vector.memset(probe[:], 0.0)
+        nc.scalar.activation(probe[:], probe[:], SILU)
+        planes = w_planes[:].rearrange("p g n -> p (g n)").bitcast(I32)
+        nc.vector.memset(planes, 0)
+        nc.gpsimd.memset(scales[:].rearrange("p a t -> p (a t)"), 0)
+        for quadrant in range(4):
+            nc.scalar.dma_start(
+                out=planes[32 * quadrant : 32 * quadrant + 4, :].rearrange("r (g n) -> r g n", g=E * PASSES),
+                in_=w_scales[:, :, 4 * quadrant : 4 * quadrant + 4, :].rearrange("e a r n -> r (e a) n").bitcast(I32),
+            )
+        nc.scalar.dma_start(out=bias[:], in_=b.rearrange("(c p) e -> p c e", p=P))
+
+        def load_x(a, t0, t1):
+            rows = xT[a * K_PASS : (a + 1) * K_PASS, :].rearrange("(p j) w -> p j w", j=PACK)
+            nc.sync.dma_start(out=raw[a][:, :, t0:t1], in_=rows[:, :, t0:t1])
+
+        def load_w(a):
+            nc.sync.dma_start(
+                out=w_codes[a][:].bitcast(I32),
+                in_=w_words[:, a].rearrange("e p c -> p e c").bitcast(I32),
+            )
+
+        for a in range(PASSES):
+            edges = LOADS[a]
+            for t0, t1 in zip(edges[:-1], edges[1:]):
+                load_x(a, t0, t1)
+            if a == 0:
+                nc.sync.dma_start(offsets[:], offs)
+            load_w(a)
+        nc.sync.dma_start(out=gates[:], in_=gate.rearrange("(c p) t -> p c t", p=P))
+
+        def cast(a, engine, t0, t1):
+            dst = grouped[a][:, t0:t1, :].rearrange("p (c i) j -> p c j i", i=4)
+            src = raw[a][:, :, t0:t1].rearrange("p j (c i) -> p c j i", i=4)
+            if engine == "v":
+                nc.vector.tensor_copy(dst, src)
+            else:
+                nc.scalar.activation(dst, src, COPY)
+
+        def quantize(a, t0, t1):
+            nc.vector.quantize_mx(
+                out=words[a][:, t0:t1].bitcast(E4M3X4),
+                scales=scales[:, a, t0:t1],
+                in_=grouped[a][:, t0:t1, :].rearrange("p t j -> p (t j)"),
+            )
+
+        def gather(a, e):
+            s0, s1 = STARTS[e], STARTS[e] + COUNTS[e]
+            lists = offsets[:, s0 // 16 : s1 // 16]
+            nc.vector.tensor_copy(slot_words[a][:, s0:s1], words[a][:].indirect(lists))
+            nc.vector.tensor_copy(slot_scales[a][:, s0:s1], scales[:, a, :].indirect(lists))
+
+        def multiply(a, e, n, s0, s1, acc):
+            nc.tensor.matmul_mx(
+                out=acc,
+                lhsT=w_codes[a][:, e, 2 * P * n : 2 * P * (n + 1)].bitcast(E2M1X4),
+                lhsT_scale=w_planes[:, e * PASSES + a, P * n : P * (n + 1)],
+                rhs=slot_words[a][:, s0:s1].bitcast(E4M3X4),
+                rhs_scale=slot_scales[a][:, s0:s1],
+                start=(a == 0),
+                stop=(a == PASSES - 1),
+            )
+
+        def activate(e, n):
+            s0, s1 = STARTS[e], STARTS[e] + COUNTS[e]
+            acc = (acc0, acc1)[e][n]
+            nc.scalar.activation(y[n][:, s0:s1], acc[:], SILU, bias=bias[:, n, e : e + 1])
+
+        def scatter(e, n):
+            s0, s1 = STARTS[e], STARTS[e] + COUNTS[e]
+            nc.vector.tensor_tensor(
+                spread[n][:].indirect(offsets[:, s0 // 16 : s1 // 16]), y[n][:, s0:s1], gates[:, n, s0:s1], MULT
+            )
+
+        for a in range(PASSES):
+            for engine, t0, t1 in CASTS[a]:
+                cast(a, engine, t0, t1)
+            for t0, t1 in QUANTS:
+                quantize(a, t0, t1)
+            gather(a, 1)
+            for n in range(N_BLOCKS):
+                multiply(a, 1, n, 256, 768, acc1[n][:])
+            gather(a, 0)
+            if a < PASSES - 1:
+                for n in range(N_BLOCKS):
+                    multiply(a, 0, n, 0, 128, acc0[n][:, 0:128])
+        for n in range(N_BLOCKS):
+            activate(1, n)
+        for n in range(N_BLOCKS):
+            multiply(PASSES - 1, 0, n, 0, 128, acc0[n][:, 0:128])
+            for a in range(PASSES):
+                multiply(a, 0, n, 128, 256, acc0[n][:, 128:256])
+            activate(0, n)
+        for n in range(N_BLOCKS):
+            scatter(1, n)
+            scatter(0, n)
+            nc.sync.dma_start(out=out[P * n : P * (n + 1), :], in_=spread[n][:, 0:T])

@@ -24,15 +24,6 @@ COPY = mybir.ActivationFunctionType.Copy
 SILU = mybir.ActivationFunctionType.Silu
 MULT = mybir.AluOpType.mult
 
-LOADS = ((0, 256, 768), (0, 768), (0, 768), (0, 512, 768))
-CASTS = (
-    (("v", 0, 256), ("s", 256, 512), ("v", 512, 768)),
-    (("s", 0, 256), ("s", 256, 512), ("s", 512, 768)),
-    (("s", 0, 256), ("s", 256, 512), ("s", 512, 768)),
-    (("s", 0, 256), ("v", 256, 512), ("v", 512, 640), ("s", 640, 768)),
-)
-QUANTS = ((0, 256), (256, 512), (512, 768))
-
 
 def tile_moe_rag_lin_silu_kernel(tc, xT, w_words, w_scales, b, gate, offs, out):
     nc = tc.nc
@@ -40,8 +31,8 @@ def tile_moe_rag_lin_silu_kernel(tc, xT, w_words, w_scales, b, gate, offs, out):
         offsets = keep.tile([P, T // 16], U16, name="offsets")
         raw = [keep.tile([P, PACK, T], F32, name="raw%d" % a, align_bytes=64) for a in range(PASSES)]
         grouped = [keep.tile([P, T, PACK], BF16, name="grouped%d" % a, align_bytes=64) for a in range(PASSES)]
-        words = [keep.tile([P, T], U32, name="words%d" % a, align_bytes=64) for a in range(PASSES)]
-        scales = keep.tile([P, PASSES, T], U8, name="scales", align_bytes=64)
+        words = keep.tile([P, PASSES, WINDOW], I32, name="words", align_bytes=64)
+        scales = keep.tile([P, PASSES, WINDOW], U8, name="scales", align_bytes=64)
         slot_words = [keep.tile([P, T], U32, name="slot_words%d" % a, align_bytes=64) for a in range(PASSES)]
         slot_scales = [keep.tile([P, T], U8, name="slot_scales%d" % a, align_bytes=64) for a in range(PASSES)]
         w_codes = [keep.tile([P, E, 2 * N], U8, name="w_codes%d" % a, align_bytes=64) for a in range(PASSES)]
@@ -50,21 +41,10 @@ def tile_moe_rag_lin_silu_kernel(tc, xT, w_words, w_scales, b, gate, offs, out):
         gates = keep.tile([P, N_BLOCKS, T], F32, name="gates")
         probe = keep.tile([P, 1], F32, name="probe")
         y = [keep.tile([P, T], F32, name="y%d" % n) for n in range(N_BLOCKS)]
+        gy = [keep.tile([P, T], F32, name="gy%d" % n) for n in range(N_BLOCKS)]
         spread = [keep.tile([P, WINDOW], F32, name="spread%d" % n) for n in range(N_BLOCKS)]
         acc0 = [psum.tile([P, COUNTS[0]], F32, name="acc0_%d" % n) for n in range(N_BLOCKS)]
         acc1 = [psum.tile([P, COUNTS[1]], F32, name="acc1_%d" % n) for n in range(N_BLOCKS)]
-
-        nc.vector.memset(probe[:], 0.0)
-        nc.scalar.activation(probe[:], probe[:], SILU)
-        planes = w_planes[:].rearrange("p g n -> p (g n)").bitcast(I32)
-        nc.vector.memset(planes, 0)
-        nc.gpsimd.memset(scales[:].rearrange("p a t -> p (a t)"), 0)
-        for quadrant in range(4):
-            nc.scalar.dma_start(
-                out=planes[32 * quadrant : 32 * quadrant + 4, :].rearrange("r (g n) -> r g n", g=E * PASSES),
-                in_=w_scales[:, :, 4 * quadrant : 4 * quadrant + 4, :].rearrange("e a r n -> r (e a) n").bitcast(I32),
-            )
-        nc.scalar.dma_start(out=bias[:], in_=b.rearrange("(c p) e -> p c e", p=P))
 
         def load_x(a, t0, t1):
             rows = xT[a * K_PASS : (a + 1) * K_PASS, :].rearrange("(p j) w -> p j w", j=PACK)
@@ -76,35 +56,62 @@ def tile_moe_rag_lin_silu_kernel(tc, xT, w_words, w_scales, b, gate, offs, out):
                 in_=w_words[:, a].rearrange("e p c -> p e c").bitcast(I32),
             )
 
-        for a in range(PASSES):
-            edges = LOADS[a]
-            for t0, t1 in zip(edges[:-1], edges[1:]):
-                load_x(a, t0, t1)
-            if a == 0:
-                nc.sync.dma_start(offsets[:], offs)
-            load_w(a)
-        nc.sync.dma_start(out=gates[:], in_=gate.rearrange("(c p) t -> p c t", p=P))
+        def load_offs():
+            nc.sync.dma_start(offsets[:], offs)
 
-        def cast(a, engine, t0, t1):
+        def load_gate():
+            nc.sync.dma_start(out=gates[:], in_=gate.rearrange("(c p) t -> p c t", p=P))
+
+        nc.vector.memset(probe[:], 0.0)
+        nc.scalar.activation(probe[:], probe[:], SILU)
+        planes = w_planes[:].rearrange("p g n -> p (g n)").bitcast(I32)
+        nc.vector.memset(planes, 0)
+        nc.gpsimd.memset(scales[:].rearrange("p a t -> p (a t)").bitcast(I32), 0)
+        nc.vector.memset(words[:, :, T:WINDOW], 0)
+        for quadrant in range(4):
+            nc.scalar.dma_start(
+                out=planes[32 * quadrant : 32 * quadrant + 4, :].rearrange("r (g n) -> r g n", g=E * PASSES),
+                in_=w_scales[:, :, 4 * quadrant : 4 * quadrant + 4, :].rearrange("e a r n -> r (e a) n").bitcast(I32),
+            )
+        nc.scalar.dma_start(out=bias[:], in_=b.rearrange("(c p) e -> p c e", p=P))
+
+        load_x(0, 0, 384)
+        load_offs()
+        load_x(0, 384, 768)
+        load_x(1, 0, 768)
+        load_x(2, 0, 768)
+        load_x(3, 0, 512)
+        load_x(3, 512, 768)
+        load_w(0)
+        load_w(1)
+        load_w(2)
+        load_w(3)
+        load_gate()
+
+        def cast_v(a, t0, t1):
             dst = grouped[a][:, t0:t1, :].rearrange("p (c i) j -> p c j i", i=4)
             src = raw[a][:, :, t0:t1].rearrange("p j (c i) -> p c j i", i=4)
-            if engine == "v":
-                nc.vector.tensor_copy(dst, src)
-            else:
-                nc.scalar.activation(dst, src, COPY)
+            nc.vector.tensor_copy(dst, src)
+
+        def cast_s(a, t0, t1):
+            dst = grouped[a][:, t0:t1, :].rearrange("p (c i) j -> p c j i", i=4)
+            src = raw[a][:, :, t0:t1].rearrange("p j (c i) -> p c j i", i=4)
+            nc.scalar.activation(dst, src, COPY)
 
         def quantize(a, t0, t1):
             nc.vector.quantize_mx(
-                out=words[a][:, t0:t1].bitcast(E4M3X4),
+                out=words[:, a, t0:t1].bitcast(E4M3X4),
                 scales=scales[:, a, t0:t1],
                 in_=grouped[a][:, t0:t1, :].rearrange("p t j -> p (t j)"),
             )
 
-        def gather(a, e):
-            s0, s1 = STARTS[e], STARTS[e] + COUNTS[e]
-            lists = offsets[:, s0 // 16 : s1 // 16]
-            nc.vector.tensor_copy(slot_words[a][:, s0:s1], words[a][:].indirect(lists))
-            nc.vector.tensor_copy(slot_scales[a][:, s0:s1], scales[:, a, :].indirect(lists))
+        def gather_words(a, s0, s1):
+            nc.vector.tensor_copy(
+                slot_words[a][:, s0:s1], words[:, a, :].bitcast(U32).indirect(offsets[:, s0 // 16 : s1 // 16])
+            )
+
+        def gather_bytes(a, s0, s1):
+            nc.vector.tensor_copy(slot_scales[a][:, s0:s1], scales[:, a, :].indirect(offsets[:, s0 // 16 : s1 // 16]))
 
         def multiply(a, e, n, s0, s1, acc):
             nc.tensor.matmul_mx(
@@ -117,37 +124,90 @@ def tile_moe_rag_lin_silu_kernel(tc, xT, w_words, w_scales, b, gate, offs, out):
                 stop=(a == PASSES - 1),
             )
 
+        def mm1(a):
+            for n in range(N_BLOCKS):
+                multiply(a, 1, n, 256, 768, acc1[n][:])
+
+        def mm0(a):
+            for n in range(N_BLOCKS):
+                multiply(a, 0, n, 0, 128, acc0[n][:, 0:128])
+
+        def mm0_last(n):
+            multiply(PASSES - 1, 0, n, 0, 128, acc0[n][:, 0:128])
+            for a in range(PASSES):
+                multiply(a, 0, n, 128, 256, acc0[n][:, 128:256])
+
         def activate(e, n):
             s0, s1 = STARTS[e], STARTS[e] + COUNTS[e]
             acc = (acc0, acc1)[e][n]
             nc.scalar.activation(y[n][:, s0:s1], acc[:], SILU, bias=bias[:, n, e : e + 1])
 
-        def scatter(e, n):
-            s0, s1 = STARTS[e], STARTS[e] + COUNTS[e]
+        def scatter(n, s0, s1):
             nc.vector.tensor_tensor(
                 spread[n][:].indirect(offsets[:, s0 // 16 : s1 // 16]), y[n][:, s0:s1], gates[:, n, s0:s1], MULT
             )
 
-        for a in range(PASSES):
-            for engine, t0, t1 in CASTS[a]:
-                cast(a, engine, t0, t1)
-            for t0, t1 in QUANTS:
-                quantize(a, t0, t1)
-            gather(a, 1)
-            for n in range(N_BLOCKS):
-                multiply(a, 1, n, 256, 768, acc1[n][:])
-            gather(a, 0)
-            if a < PASSES - 1:
-                for n in range(N_BLOCKS):
-                    multiply(a, 0, n, 0, 128, acc0[n][:, 0:128])
+        def mult_v(n, s0, s1):
+            nc.vector.tensor_tensor(gy[n][:, s0:s1], y[n][:, s0:s1], gates[:, n, s0:s1], MULT)
+
+        def mult_g(n, s0, s1):
+            nc.gpsimd.tensor_tensor(gy[n][:, s0:s1], y[n][:, s0:s1], gates[:, n, s0:s1], MULT)
+
+        def scatter_copy(n, s0, s1):
+            nc.vector.tensor_copy(spread[n][:].indirect(offsets[:, s0 // 16 : s1 // 16]), gy[n][:, s0:s1])
+
+        def store(n):
+            nc.sync.dma_start(out=out[P * n : P * (n + 1), :], in_=spread[n][:, 0:T])
+
+        cast_v(0, 0, 128)
+        cast_s(0, 128, 384)
+        cast_v(0, 384, 640)
+        cast_s(0, 640, 768)
+        quantize(0, 0, 512)
+        quantize(0, 512, 768)
+        gather_words(0, 0, 768)
+        cast_v(1, 0, 128)
+        cast_s(1, 128, 512)
+        cast_s(1, 512, 768)
+        gather_bytes(0, 0, 768)
+        mm1(0)
+        mm0(0)
+        quantize(1, 0, 512)
+        quantize(1, 512, 768)
+        gather_words(1, 0, 768)
+        cast_v(2, 0, 128)
+        cast_s(2, 128, 512)
+        cast_s(2, 512, 768)
+        gather_bytes(1, 0, 768)
+        mm1(1)
+        mm0(1)
+        quantize(2, 0, 512)
+        quantize(2, 512, 768)
+        gather_words(2, 0, 768)
+        cast_s(3, 0, 256)
+        cast_s(3, 256, 512)
+        cast_s(3, 512, 768)
+        gather_bytes(2, 0, 768)
+        mm1(2)
+        mm0(2)
+        quantize(3, 0, 512)
+        quantize(3, 512, 768)
+        gather_words(3, 256, 768)
+        gather_bytes(3, 256, 768)
+        mm1(3)
         for n in range(N_BLOCKS):
             activate(1, n)
+        gather_words(3, 0, 256)
+        gather_bytes(3, 0, 256)
         for n in range(N_BLOCKS):
-            multiply(PASSES - 1, 0, n, 0, 128, acc0[n][:, 0:128])
-            for a in range(PASSES):
-                multiply(a, 0, n, 128, 256, acc0[n][:, 128:256])
+            mm0_last(n)
             activate(0, n)
-        for n in range(N_BLOCKS):
-            scatter(1, n)
-            scatter(0, n)
-            nc.sync.dma_start(out=out[P * n : P * (n + 1), :], in_=spread[n][:, 0:T])
+        scatter(0, 256, 768)
+        scatter(1, 256, 768)
+        scatter(0, 0, 256)
+        store(0)
+        scatter(2, 256, 768)
+        scatter(1, 0, 256)
+        store(1)
+        scatter(2, 0, 256)
+        store(2)

@@ -59,8 +59,8 @@ def tile_moe_rag_lin_silu_kernel(tc, xT, w_words, w_scales, b, gate, offs, out):
         def load_offs():
             nc.sync.dma_start(offsets[:], offs)
 
-        def load_gate():
-            nc.sync.dma_start(out=gates[:], in_=gate.rearrange("(c p) t -> p c t", p=P))
+        def load_gate(n):
+            nc.sync.dma_start(out=gates[:, n, :], in_=gate[P * n : P * (n + 1), :])
 
         nc.vector.memset(probe[:], 0.0)
         nc.scalar.activation(probe[:], probe[:], SILU)
@@ -75,18 +75,19 @@ def tile_moe_rag_lin_silu_kernel(tc, xT, w_words, w_scales, b, gate, offs, out):
             )
         nc.scalar.dma_start(out=bias[:], in_=b.rearrange("(c p) e -> p c e", p=P))
 
-        load_x(0, 0, 384)
+        load_x(0, 0, 768)
         load_offs()
-        load_x(0, 384, 768)
         load_x(1, 0, 768)
         load_x(2, 0, 768)
+        load_w(0)
         load_x(3, 0, 512)
         load_x(3, 512, 768)
-        load_w(0)
         load_w(1)
         load_w(2)
         load_w(3)
-        load_gate()
+        load_gate(0)
+        load_gate(1)
+        load_gate(2)
 
         def cast_v(a, t0, t1):
             dst = grouped[a][:, t0:t1, :].rearrange("p (c i) j -> p c j i", i=4)
@@ -159,15 +160,14 @@ def tile_moe_rag_lin_silu_kernel(tc, xT, w_words, w_scales, b, gate, offs, out):
         def store(n):
             nc.sync.dma_start(out=out[P * n : P * (n + 1), :], in_=spread[n][:, 0:T])
 
-        cast_v(0, 0, 128)
-        cast_s(0, 128, 384)
-        cast_v(0, 384, 640)
-        cast_s(0, 640, 768)
+        cast_v(0, 0, 384)
+        cast_s(0, 384, 512)
+        cast_s(0, 512, 768)
         quantize(0, 0, 512)
         quantize(0, 512, 768)
         gather_words(0, 0, 768)
-        cast_v(1, 0, 128)
-        cast_s(1, 128, 512)
+        cast_v(1, 0, 256)
+        cast_s(1, 256, 512)
         cast_s(1, 512, 768)
         gather_bytes(0, 0, 768)
         mm1(0)
@@ -184,30 +184,30 @@ def tile_moe_rag_lin_silu_kernel(tc, xT, w_words, w_scales, b, gate, offs, out):
         quantize(2, 0, 512)
         quantize(2, 512, 768)
         gather_words(2, 0, 768)
-        cast_s(3, 0, 256)
-        cast_s(3, 256, 512)
-        cast_s(3, 512, 768)
         gather_bytes(2, 0, 768)
         mm1(2)
         mm0(2)
+        cast_s(3, 0, 256)
+        cast_s(3, 256, 512)
+        cast_s(3, 512, 768)
         quantize(3, 0, 512)
         quantize(3, 512, 768)
-        gather_words(3, 256, 768)
-        gather_bytes(3, 256, 768)
-        mm1(3)
-        for n in range(N_BLOCKS):
-            activate(1, n)
         gather_words(3, 0, 256)
         gather_bytes(3, 0, 256)
         for n in range(N_BLOCKS):
             mm0_last(n)
             activate(0, n)
-        scatter(0, 256, 768)
-        scatter(1, 256, 768)
+        gather_words(3, 256, 768)
+        gather_bytes(3, 256, 768)
+        mm1(3)
+        for n in range(N_BLOCKS):
+            activate(1, n)
         scatter(0, 0, 256)
-        store(0)
-        scatter(2, 256, 768)
         scatter(1, 0, 256)
-        store(1)
+        scatter(0, 256, 768)
+        store(0)
         scatter(2, 0, 256)
+        scatter(1, 256, 768)
+        store(1)
+        scatter(2, 256, 768)
         store(2)

import concourse.mybir as mybir

K, T, E, N = 2048, 768, 2, 384
COUNTS = (256, 512)
STARTS = (0, 256)
FLOPS = 2 * T * K * N

P = 128
PACK = 4
K_PASS = P * PACK
PASSES = K // K_PASS
N_BLOCKS = N // P
WINDOW = 1024

F32 = mybir.dt.float32
BF16 = mybir.dt.bfloat16
I32 = mybir.dt.int32
U32 = mybir.dt.uint32
U16 = mybir.dt.uint16
U8 = mybir.dt.uint8
E4M3X4 = mybir.dt.float8_e4m3fn_x4
E2M1X4 = mybir.dt.float4_e2m1fn_x4
COPY = mybir.ActivationFunctionType.Copy
SILU = mybir.ActivationFunctionType.Silu
MULT = mybir.AluOpType.mult


def tile_moe_rag_lin_silu_kernel(tc, xT, w_words, w_scales, b, gate, offs, out):
    nc = tc.nc
    with tc.tile_pool(name="keep", bufs=1) as keep, tc.psum_pool(name="psum", bufs=1) as psum:
        offsets = keep.tile([P, T // 16], U16, name="offsets")
        raw = [keep.tile([P, PACK, T], F32, name="raw%d" % a, align_bytes=64) for a in range(PASSES)]
        grouped = [keep.tile([P, T, PACK], BF16, name="grouped%d" % a, align_bytes=64) for a in range(PASSES)]
        words = keep.tile([P, PASSES, WINDOW], I32, name="words", align_bytes=64)
        scales = keep.tile([P, PASSES, WINDOW], U8, name="scales", align_bytes=64)
        slot_words = [keep.tile([P, T], U32, name="slot_words%d" % a, align_bytes=64) for a in range(PASSES)]
        slot_scales = [keep.tile([P, T], U8, name="slot_scales%d" % a, align_bytes=64) for a in range(PASSES)]
        w_codes = [keep.tile([P, E, 2 * N], U8, name="w_codes%d" % a, align_bytes=64) for a in range(PASSES)]
        w_planes = keep.tile([P, E * PASSES, N], U8, name="w_planes", align_bytes=64)
        bias = keep.tile([P, N_BLOCKS, E], F32, name="bias")
        gates = keep.tile([P, N_BLOCKS, T], F32, name="gates")
        probe = keep.tile([P, 1], F32, name="probe")
        y = [keep.tile([P, T], F32, name="y%d" % n) for n in range(N_BLOCKS)]
        gy = [keep.tile([P, T], F32, name="gy%d" % n) for n in range(N_BLOCKS)]
        spread = [keep.tile([P, WINDOW], F32, name="spread%d" % n) for n in range(N_BLOCKS)]
        acc0 = [psum.tile([P, COUNTS[0]], F32, name="acc0_%d" % n) for n in range(N_BLOCKS)]
        acc1 = [psum.tile([P, COUNTS[1]], F32, name="acc1_%d" % n) for n in range(N_BLOCKS)]

        def load_x(a, t0, t1):
            rows = xT[a * K_PASS : (a + 1) * K_PASS, :].rearrange("(p j) w -> p j w", j=PACK)
            nc.sync.dma_start(out=raw[a][:, :, t0:t1], in_=rows[:, :, t0:t1])

        def load_w(a):
            nc.sync.dma_start(
                out=w_codes[a][:].bitcast(I32),
                in_=w_words[:, a].rearrange("e p c -> p e c").bitcast(I32),
            )

        def load_offs():
            nc.sync.dma_start(offsets[:], offs)

        def load_gate(n):
            nc.sync.dma_start(out=gates[:, n, :], in_=gate[P * n : P * (n + 1), :])

        nc.vector.memset(probe[:], 0.0)
        nc.scalar.activation(probe[:], probe[:], SILU)
        planes = w_planes[:].rearrange("p g n -> p (g n)").bitcast(I32)
        nc.vector.memset(planes, 0)
        nc.gpsimd.memset(scales[:].rearrange("p a t -> p (a t)").bitcast(I32), 0)
        nc.vector.memset(words[:, :, T:WINDOW], 0)
        for quadrant in range(4):
            nc.scalar.dma_start(
                out=planes[32 * quadrant : 32 * quadrant + 4, :].rearrange("r (g n) -> r g n", g=E * PASSES),
                in_=w_scales[:, :, 4 * quadrant : 4 * quadrant + 4, :].rearrange("e a r n -> r (e a) n").bitcast(I32),
            )
        nc.scalar.dma_start(out=bias[:], in_=b.rearrange("(c p) e -> p c e", p=P))

        load_x(0, 0, 768)
        load_offs()
        load_x(1, 0, 768)
        load_x(2, 0, 768)
        load_w(0)
        load_x(3, 0, 512)
        load_x(3, 512, 768)
        load_w(1)
        load_w(2)
        load_w(3)
        load_gate(0)
        load_gate(1)
        load_gate(2)

        def cast_v(a, t0, t1):
            dst = grouped[a][:, t0:t1, :].rearrange("p (c i) j -> p c j i", i=4)
            src = raw[a][:, :, t0:t1].rearrange("p j (c i) -> p c j i", i=4)
            nc.vector.tensor_copy(dst, src)

        def cast_s(a, t0, t1):
            dst = grouped[a][:, t0:t1, :].rearrange("p (c i) j -> p c j i", i=4)
            src = raw[a][:, :, t0:t1].rearrange("p j (c i) -> p c j i", i=4)
            nc.scalar.activation(dst, src, COPY)

        def quantize(a, t0, t1):
            nc.vector.quantize_mx(
                out=words[:, a, t0:t1].bitcast(E4M3X4),
                scales=scales[:, a, t0:t1],
                in_=grouped[a][:, t0:t1, :].rearrange("p t j -> p (t j)"),
            )

        def gather_words(a, s0, s1):
            nc.vector.tensor_copy(
                slot_words[a][:, s0:s1], words[:, a, :].bitcast(U32).indirect(offsets[:, s0 // 16 : s1 // 16])
            )

        def gather_bytes(a, s0, s1):
            nc.vector.tensor_copy(slot_scales[a][:, s0:s1], scales[:, a, :].indirect(offsets[:, s0 // 16 : s1 // 16]))

        def multiply(a, e, n, s0, s1, acc):
            nc.tensor.matmul_mx(
                out=acc,
                lhsT=w_codes[a][:, e, 2 * P * n : 2 * P * (n + 1)].bitcast(E2M1X4),
                lhsT_scale=w_planes[:, e * PASSES + a, P * n : P * (n + 1)],
                rhs=slot_words[a][:, s0:s1].bitcast(E4M3X4),
                rhs_scale=slot_scales[a][:, s0:s1],
                start=(a == 0),
                stop=(a == PASSES - 1),
            )

        def mm1(a):
            for n in range(N_BLOCKS):
                multiply(a, 1, n, 256, 768, acc1[n][:])

        def mm0(a):
            for n in range(N_BLOCKS):
                multiply(a, 0, n, 0, 128, acc0[n][:, 0:128])

        def mm0_last(n):
            multiply(PASSES - 1, 0, n, 0, 128, acc0[n][:, 0:128])
            for a in range(PASSES):
                multiply(a, 0, n, 128, 256, acc0[n][:, 128:256])

        def activate(e, n):
            s0, s1 = STARTS[e], STARTS[e] + COUNTS[e]
            acc = (acc0, acc1)[e][n]
            nc.scalar.activation(y[n][:, s0:s1], acc[:], SILU, bias=bias[:, n, e : e + 1])

        def scatter(n, s0, s1):
            nc.vector.tensor_tensor(
                spread[n][:].indirect(offsets[:, s0 // 16 : s1 // 16]), y[n][:, s0:s1], gates[:, n, s0:s1], MULT
            )

        def mult_v(n, s0, s1):
            nc.vector.tensor_tensor(gy[n][:, s0:s1], y[n][:, s0:s1], gates[:, n, s0:s1], MULT)

        def mult_g(n, s0, s1):
            nc.gpsimd.tensor_tensor(gy[n][:, s0:s1], y[n][:, s0:s1], gates[:, n, s0:s1], MULT)

        def scatter_copy(n, s0, s1):
            nc.vector.tensor_copy(spread[n][:].indirect(offsets[:, s0 // 16 : s1 // 16]), gy[n][:, s0:s1])

        def store(n):
            nc.sync.dma_start(out=out[P * n : P * (n + 1), :], in_=spread[n][:, 0:T])

        cast_v(0, 0, 384)
        cast_s(0, 384, 512)
        cast_s(0, 512, 768)
        quantize(0, 0, 512)
        quantize(0, 512, 768)
        gather_words(0, 0, 768)
        cast_v(1, 0, 256)
        cast_s(1, 256, 512)
        cast_s(1, 512, 768)
        gather_bytes(0, 0, 768)
        mm1(0)
        mm0(0)
        quantize(1, 0, 512)
        quantize(1, 512, 768)
        gather_words(1, 0, 768)
        cast_v(2, 0, 128)
        cast_s(2, 128, 512)
        cast_s(2, 512, 768)
        gather_bytes(1, 0, 768)
        mm1(1)
        mm0(1)
        quantize(2, 0, 512)
        quantize(2, 512, 768)
        gather_words(2, 0, 768)
        gather_bytes(2, 0, 768)
        mm1(2)
        mm0(2)
        cast_s(3, 0, 256)
        cast_s(3, 256, 512)
        cast_s(3, 512, 768)
        quantize(3, 0, 512)
        quantize(3, 512, 768)
        gather_words(3, 0, 256)
        gather_bytes(3, 0, 256)
        for n in range(N_BLOCKS):
            mm0_last(n)
            activate(0, n)
        gather_words(3, 256, 768)
        gather_bytes(3, 256, 768)
        mm1(3)
        for n in range(N_BLOCKS):
            activate(1, n)
        scatter(0, 0, 256)
        scatter(1, 0, 256)
        scatter(0, 256, 768)
        store(0)
        scatter(2, 0, 256)
        scatter(1, 256, 768)
        store(1)
        scatter(2, 256, 768)
        store(2)
